import numpy as np
import ml_dtypes


def mxq(x, axis, fmt="e4m3"):
    dtype, down = {"e4m3": (ml_dtypes.float8_e4m3fn, 7), "e5m2": (ml_dtypes.float8_e5m2, 14)}[fmt]
    v = np.moveaxis(np.asarray(x, np.float32).astype(ml_dtypes.bfloat16).astype(np.float64), axis, -1)
    blocks = v.reshape(v.shape[:-1] + (-1, 32))
    amax = np.abs(blocks).max(-1, keepdims=True)
    byte = np.maximum(np.where(amax > 0, np.frexp(amax)[1] - 1 + 127, 0) - down, 1)
    scale = np.exp2(byte - 127.0)
    codes = (blocks / scale).astype(np.float32).astype(dtype).astype(np.float64)
    return np.moveaxis((codes * scale).reshape(v.shape), -1, axis)


WIDE = False


def mx_kscale(k):
    if not WIDE:
        return np.ones(k)
    levels = np.array([10, -10, 5, -5, 0])
    if k % 512:
        return np.exp2(np.random.permutation(np.resize(levels, k // 32))).repeat(32)
    a = np.empty((k // 512, 16))
    for p in range(k // 512):
        a[p, :8] = np.random.permutation(np.resize(levels, 8))
        for g in range(8):
            far = levels[np.abs(levels - a[p, g]) >= 10]
            a[p, g + 8] = far[np.random.randint(len(far))]
    return np.exp2(a.ravel()).repeat(32)


BF16 = ml_dtypes.bfloat16


def bf(x):
    return np.asarray(x, np.float32).astype(BF16)


def f64(x):
    return np.asarray(x).astype(np.float64)


E2M1 = np.array([0.0, 0.5, 1.0, 1.5, 2.0, 3.0, 4.0, 6.0, -0.0, -0.5, -1.0, -1.5, -2.0, -3.0, -4.0, -6.0])


def pack_weight(w, fmt):
    k, n = w.shape
    w = f64(bf(w)).reshape(k // 32, 32, n)
    amax = np.abs(w).max(1)
    if fmt == "e4m3":
        byte = np.frexp(amax)[1] - 1 + 127 - 7
    else:
        mant, ex = np.frexp(amax / 6.0)
        byte = np.where(mant > 0.5, ex, ex - 1) + 127
    byte = np.clip(np.where(amax > 0, byte, 1), 1, 254)
    scaled = (w * np.exp2(127.0 - byte)[:, None, :]).reshape(k, n).astype(np.float32)
    by_word = np.ascontiguousarray(scaled.reshape(k // 512, 128, 4, n).transpose(0, 1, 3, 2))
    if fmt == "e4m3":
        words = by_word.astype(ml_dtypes.float8_e4m3fn).view(np.uint8)
    else:
        c = by_word.astype(ml_dtypes.float4_e2m1fn).view(np.uint8) & 0xF
        words = c[..., 0::2] | (c[..., 1::2] << 4)
    return np.ascontiguousarray(words), np.ascontiguousarray(byte.astype(np.uint8).reshape(k // 512, 16, n))


def unpack_weight(words, scales, fmt):
    g, p, n, _ = words.shape
    if fmt == "e4m3":
        vals = np.ascontiguousarray(words).view(ml_dtypes.float8_e4m3fn).astype(np.float64)
    else:
        nib = np.empty((g, p, n, 4), np.uint8)
        nib[..., 0::2] = words & 0xF
        nib[..., 1::2] = words >> 4
        vals = E2M1[nib]
    vals = vals * np.repeat(np.exp2(scales.astype(np.float64) - 127.0), 8, axis=1)[..., None]
    return vals.transpose(0, 1, 3, 2).reshape(g * 512, n)
def pack4(w):
    words, scales = pack_weight(w, "e2m1")
    return words.reshape(words.shape[0], 128, -1), scales


def unpack4(words, scales):
    return unpack_weight(words.reshape(words.shape[0], 128, -1, 2), scales, "e2m1")


M, K, N, R = 512, 2048, 3072, 512

FIX = 0.6


def setup_inputs():
    s, t = mx_kscale(K), mx_kscale(R)
    xt = np.random.standard_normal((K, M)) * s[:, None]
    w = np.random.standard_normal((K, N)) / np.sqrt(K) / s[:, None]
    a = np.random.standard_normal((K, R)) / np.sqrt(K) / s[:, None] * t
    b = FIX * np.random.standard_normal((R, N)) / np.sqrt(R) / t[:, None]
    x_words, x_scales = pack4(xt)
    w_words, w_scales = pack4(w)
    a_words, a_scales = pack4(a)
    b_words, b_scales = pack_weight(b, "e4m3")
    return {"x_words": x_words, "x_scales": x_scales,
            "w_words": w_words, "w_scales": w_scales,
            "a_words": a_words, "a_scales": a_scales,
            "b_words": b_words, "b_scales": b_scales,
            "sigma": bf(np.exp(0.3 * np.random.standard_normal(R))),
            "alpha": bf(np.random.uniform(0.5, 1.5, M)),
            "bias": bf(0.3 * np.random.standard_normal(N))}


def reference(x_words, x_scales, w_words, w_scales, a_words, a_scales, b_words, b_scales, sigma, alpha, bias):
    xt = unpack4(x_words, x_scales)
    w = unpack4(w_words, w_scales)
    a = unpack4(a_words, a_scales)
    b = unpack_weight(b_words, b_scales, "e4m3")
    base = xt.T @ w
    low = xt.T @ a
    z = low * f64(sigma) * f64(alpha)[:, None]
    fix = mxq(z, 1, "e4m3") @ b
    return base + fix + f64(bias)

@@ -1,0 +1,225 @@
+from contextlib import ExitStack
+
+import concourse.mybir as mybir
+
+M, K, N, R = 512, 2048, 3072, 512
+FLOPS = 2 * M * K * N + 2 * M * K * R + 2 * M * R * N
+
+F32 = mybir.dt.float32
+BF16 = mybir.dt.bfloat16
+I32 = mybir.dt.int32
+U32 = mybir.dt.uint32
+U8 = mybir.dt.uint8
+FP4X4 = mybir.dt.float4_e2m1fn_x4
+FP8X4 = mybir.dt.float8_e4m3fn_x4
+ALU = mybir.AluOpType
+
+P = 128
+PACK = 4
+PASSES = K // (P * PACK)
+TOKEN_TILES = M // P
+BANK = 512
+CHUNKS = N // BANK
+HALF = M // 2
+
+
+def tile_fp4_base_lowrank_fix_s4_kernel(
+    tc, x_words, x_scales, w_words, w_scales, a_words, a_scales, b_words, b_scales, sigma, alpha, bias, out
+):
+    nc = tc.nc
+
+    with ExitStack() as ctx:
+        keep = ctx.enter_context(tc.tile_pool(name="keep", bufs=1))
+        stage = ctx.enter_context(tc.tile_pool(name="stage", bufs=10))
+        psum = ctx.enter_context(tc.psum_pool(name="psum", bufs=1))
+        ctx.enter_context(tc.manual_schedule())
+
+        def scale_plane(name, passes, width):
+            plane = keep.tile([P, passes, width], U8, name=name, align_bytes=256)
+            nc.vector.memset(plane[:].bitcast(I32), 0)
+            return plane
+
+        def load_scales(plane, scales, col0):
+            width = plane.shape[2]
+            rows = scales[:, :, col0 : col0 + width].bitcast(I32).rearrange("g (q r) n -> r q g n", r=4)
+            for r in range(4):
+                nc.sync.dma_start(out=plane[r:P:32, :, :].bitcast(I32), in_=rows[r])
+
+        def load_fp4(name, words, g0, g1, col0, width):
+            codes = keep.tile([P, g1 - g0, 2 * width], U8, name=name, align_bytes=256)
+            src = words[g0:g1, :, 2 * col0 : 2 * (col0 + width)].bitcast(I32).rearrange("g p n -> p g n")
+            nc.sync.dma_start(out=codes[:].bitcast(I32), in_=src)
+            return [codes[:, g, :] for g in range(g1 - g0)]
+
+        def load_b(name, col0, width):
+            codes = keep.tile([P, width], U32, name=name, align_bytes=256)
+            src = b_words[0].rearrange("p n t -> p (n t)")[:, 4 * col0 : 4 * (col0 + width)].bitcast(I32)
+            nc.sync.dma_start(out=codes[:].bitcast(I32), in_=src)
+            return [codes[:, c : c + BANK] for c in range(0, width, BANK)]
+
+        def load_spread(name, vector, col0, width):
+            spread = keep.tile([P, width], BF16, name=name, align_bytes=256)
+            nc.sync.dma_start(out=spread[:], in_=vector[col0 : col0 + width].partition_broadcast(P))
+            return spread
+
+        x_plane = scale_plane("x_plane", PASSES, M)
+        w_plane0 = scale_plane("w_plane0", PASSES, BANK)
+        a_plane_raw = scale_plane("a_plane_raw", PASSES, R)
+        w_plane1 = scale_plane("w_plane1", PASSES, BANK)
+        b_plane = scale_plane("b_plane", 1, N)
+        w_plane_rest = scale_plane("w_plane_rest", PASSES, N - 2 * BANK)
+
+        x_codes = load_fp4("x_codes0", x_words, 0, 1, 0, M)
+        w_codes = [load_fp4("w_codes00", w_words, 0, 1, 0, BANK)]
+        load_scales(x_plane, x_scales, 0)
+        load_scales(w_plane0, w_scales, 0)
+        x_codes.extend(load_fp4("x_codes1", x_words, 1, 2, 0, M))
+        w_codes[0].extend(load_fp4("w_codes01", w_words, 1, 2, 0, BANK))
+        x_codes.extend(load_fp4("x_codes2", x_words, 2, PASSES, 0, M))
+        w_codes[0].extend(load_fp4("w_codes02", w_words, 2, PASSES, 0, BANK))
+
+        a_raw = keep.tile([P, PASSES, 2 * R], U8, name="a_raw", align_bytes=256)
+        nc.sync.dma_start(out=a_raw[:].bitcast(I32), in_=a_words.bitcast(I32).rearrange("g p n -> p g n"))
+        load_scales(a_plane_raw, a_scales, 0)
+        sigma_bf = keep.tile([P, PACK], BF16, name="sigma_bf")
+        nc.sync.dma_start(out=sigma_bf[:], in_=sigma.rearrange("(p t) -> p t", t=PACK))
+        alpha_all = load_spread("alpha_all", alpha, 0, M)
+
+        w_codes.append(load_fp4("w_codes1", w_words, 0, PASSES, BANK, BANK))
+        load_scales(w_plane1, w_scales, BANK)
+        b_codes = load_b("b_codes0", 0, 2 * BANK)
+        load_scales(b_plane, b_scales, 0)
+        bias_head = load_spread("bias_head", bias, 0, 2 * BANK)
+        load_scales(w_plane_rest, w_scales, 2 * BANK)
+        w_codes.append(load_fp4("w_codes2", w_words, 0, PASSES, 2 * BANK, BANK))
+        b_codes.extend(load_b("b_codes2", 2 * BANK, 2 * BANK))
+        bias_rest = load_spread("bias_rest", bias, 2 * BANK, N - 2 * BANK)
+        w_codes.append(load_fp4("w_codes3", w_words, 0, PASSES, 3 * BANK, BANK))
+        w_codes.append(load_fp4("w_codes4", w_words, 0, PASSES, 4 * BANK, BANK))
+        b_codes.extend(load_b("b_codes4", 4 * BANK, 2 * BANK))
+        w_codes.append(load_fp4("w_codes5", w_words, 0, PASSES, 5 * BANK, BANK))
+
+        def w_scale(n, g):
+            if n == 0:
+                return w_plane0[:, g, :]
+            if n == 1:
+                return w_plane1[:, g, :]
+            return w_plane_rest[:, g, (n - 2) * BANK : (n - 1) * BANK]
+
+        def bias_cols(n):
+            if n < 2:
+                return bias_head[:, n * BANK : (n + 1) * BANK]
+            return bias_rest[:, (n - 2) * BANK : (n - 1) * BANK]
+
+        def bank(index):
+            return psum.tile([P, BANK], F32, name="bank%d" % index, tag="bank%d" % index)
+
+        def base_pass(acc, n, m, g, c0, c1):
+            nc.tensor.matmul_mx(
+                out=acc[:, 0 : c1 - c0],
+                lhsT=x_codes[g][:, 2 * m * P : 2 * (m + 1) * P].bitcast(FP4X4),
+                lhsT_scale=x_plane[:, g, m * P : (m + 1) * P],
+                rhs=w_codes[n][g][:, 2 * c0 : 2 * c1].bitcast(FP4X4),
+                rhs_scale=w_scale(n, g)[:, c0:c1],
+                start=(g == 0),
+                stop=False,
+            )
+
+        accs = {}
+        for m in range(TOKEN_TILES):
+            accs[0, m] = bank(m)
+        for g in range(PASSES):
+            for m in range(TOKEN_TILES):
+                base_pass(accs[0, m], 0, m, g, 0, BANK)
+
+        sigma_col = keep.tile([P, PACK], F32, name="sigma_col")
+        a_codes, a_planes = [], []
+        for t in range(PACK):
+            codes = keep.tile([P, PASSES, P, 2], U8, name="a_codes%d" % t, align_bytes=256)
+            plane = keep.tile([P, PASSES, P], U8, name="a_plane%d" % t, align_bytes=256)
+            nc.vector.tensor_copy(
+                out=codes[:], in_=a_raw[:].rearrange("p g (m t b) -> p t g m b", t=PACK, b=2)[:, t]
+            )
+            nc.vector.tensor_copy(
+                out=plane[:], in_=a_plane_raw[:].rearrange("p g (m t) -> p t g m", t=PACK)[:, t]
+            )
+            a_codes.append(codes)
+            a_planes.append(plane)
+        nc.vector.tensor_copy(out=sigma_col[:], in_=sigma_bf[:])
+
+        z_rows = keep.tile([P, PACK, M], BF16, name="z_rows", align_bytes=256)
+        for t in range(PACK):
+            low = bank(TOKEN_TILES + t)
+            for g in range(PASSES):
+                nc.tensor.matmul_mx(
+                    out=low[:],
+                    lhsT=a_codes[t][:, g].rearrange("p m b -> p (m b)").bitcast(FP4X4),
+                    lhsT_scale=a_planes[t][:, g, :],
+                    rhs=x_codes[g].bitcast(FP4X4),
+                    rhs_scale=x_plane[:, g, :],
+                    start=(g == 0),
+                    stop=(g == PASSES - 1),
+                )
+            nc.vector.scalar_tensor_tensor(
+                out=z_rows[:, t, :],
+                in0=low[:],
+                scalar=sigma_col[:, t : t + 1],
+                in1=alpha_all[:],
+                op0=ALU.mult,
+                op1=ALU.mult,
+            )
+
+        z_grouped, z_codes, z_planes = [], [], []
+        for h in range(2):
+            grouped = keep.tile([P, HALF, PACK], BF16, name="z_grouped%d" % h, align_bytes=256)
+            nc.vector.tensor_copy(
+                out=grouped[:].rearrange("p (c i) t -> p c t i", i=4),
+                in_=z_rows[:, :, h * HALF : (h + 1) * HALF].rearrange("p t (c i) -> p c t i", i=4),
+            )
+            z_grouped.append(grouped)
+        for h in range(2):
+            codes = keep.tile([P, HALF], U32, name="z_codes%d" % h, align_bytes=256)
+            plane = keep.tile([P, HALF], U8, name="z_plane%d" % h, align_bytes=256)
+            nc.vector.quantize_mx(
+                out=codes[:].bitcast(FP8X4),
+                scales=plane[:],
+                in_=z_grouped[h][:].rearrange("p c t -> p (c t)"),
+            )
+            z_codes.append(codes)
+            z_planes.append(plane)
+
+        def finish(acc, n, m, c0, c1):
+            h, col = divmod(m * P, HALF)
+            nc.tensor.matmul_mx(
+                out=acc[:, 0 : c1 - c0],
+                lhsT=z_codes[h][:, col : col + P].bitcast(FP8X4),
+                lhsT_scale=z_planes[h][:, col : col + P],
+                rhs=b_codes[n][:, c0:c1].bitcast(FP8X4),
+                rhs_scale=b_plane[:, 0, n * BANK + c0 : n * BANK + c1],
+                start=False,
+                stop=True,
+            )
+            result = stage.tile([P, BANK], F32, name="result", tag="result")
+            nc.vector.tensor_tensor(
+                out=result[:, 0 : c1 - c0], in0=acc[:, 0 : c1 - c0], in1=bias_cols(n)[:, c0:c1], op=ALU.add
+            )
+            nc.scalar.dma_start(
+                out=out[m * P : (m + 1) * P, n * BANK + c0 : n * BANK + c1], in_=result[:, 0 : c1 - c0]
+            )
+
+        for m in range(TOKEN_TILES):
+            accs[1, m] = bank(TOKEN_TILES + m)
+            for g in range(PASSES):
+                base_pass(accs[1, m], 1, m, g, 0, BANK)
+        for n in range(2):
+            for m in range(TOKEN_TILES):
+                finish(accs[n, m], n, m, 0, BANK)
+
+        pieces = [(n, m, 0, BANK) for n in range(2, CHUNKS) for m in range(TOKEN_TILES)]
+        n, m = pieces[-1][0], pieces[-1][1]
+        pieces = pieces[:-1] + [(n, m, 0, BANK // 2), (n, m, BANK // 2, BANK)]
+        for index, (n, m, c0, c1) in enumerate(pieces):
+            acc = bank(index % 8)
+            for g in range(PASSES):
+                base_pass(acc, n, m, g, c0, c1)
+            finish(acc, n, m, c0, c1)

@@ -70,8 +70,8 @@ def tile_fp4_base_lowrank_fix_s4_kernel(
         w_plane_rest = scale_plane("w_plane_rest", PASSES, N - 2 * BANK)
 
         x_codes = load_fp4("x_codes0", x_words, 0, 1, 0, M)
-        w_codes = [load_fp4("w_codes00", w_words, 0, 1, 0, BANK)]
         load_scales(x_plane, x_scales, 0)
+        w_codes = [load_fp4("w_codes00", w_words, 0, 1, 0, BANK)]
         load_scales(w_plane0, w_scales, 0)
         x_codes.extend(load_fp4("x_codes1", x_words, 1, 2, 0, M))
         w_codes[0].extend(load_fp4("w_codes01", w_words, 1, 2, 0, BANK))
@@ -203,7 +203,7 @@ def tile_fp4_base_lowrank_fix_s4_kernel(
             nc.vector.tensor_tensor(
                 out=result[:, 0 : c1 - c0], in0=acc[:, 0 : c1 - c0], in1=bias_cols(n)[:, c0:c1], op=ALU.add
             )
-            nc.scalar.dma_start(
+            nc.sync.dma_start(
                 out=out[m * P : (m + 1) * P, n * BANK + c0 : n * BANK + c1], in_=result[:, 0 : c1 - c0]
             )
 
@@ -217,7 +217,7 @@ def tile_fp4_base_lowrank_fix_s4_kernel(
 
         pieces = [(n, m, 0, BANK) for n in range(2, CHUNKS) for m in range(TOKEN_TILES)]
         n, m = pieces[-1][0], pieces[-1][1]
-        pieces = pieces[:-1] + [(n, m, 0, BANK // 2), (n, m, BANK // 2, BANK)]
+        pieces = pieces[:-1] + [(n, m, 0, 256), (n, m, 256, 384), (n, m, 384, 512)]
         for index, (n, m, c0, c1) in enumerate(pieces):
             acc = bank(index % 8)
             for g in range(PASSES):

@@ -30,7 +30,7 @@ def tile_fp4_base_lowrank_fix_s4_kernel(
 
     with ExitStack() as ctx:
         keep = ctx.enter_context(tc.tile_pool(name="keep", bufs=1))
-        stage = ctx.enter_context(tc.tile_pool(name="stage", bufs=10))
+        stage = ctx.enter_context(tc.tile_pool(name="stage", bufs=16))
         psum = ctx.enter_context(tc.psum_pool(name="psum", bufs=1))
         ctx.enter_context(tc.manual_schedule())
 
@@ -67,11 +67,12 @@ def tile_fp4_base_lowrank_fix_s4_kernel(
         a_plane_raw = scale_plane("a_plane_raw", PASSES, R)
         w_plane1 = scale_plane("w_plane1", PASSES, BANK)
         b_plane = scale_plane("b_plane", 1, N)
-        w_plane_rest = scale_plane("w_plane_rest", PASSES, N - 2 * BANK)
+        w_plane2 = scale_plane("w_plane2", PASSES, BANK)
+        w_plane_rest = scale_plane("w_plane_rest", PASSES, N - 3 * BANK)
 
         x_codes = load_fp4("x_codes0", x_words, 0, 1, 0, M)
-        load_scales(x_plane, x_scales, 0)
         w_codes = [load_fp4("w_codes00", w_words, 0, 1, 0, BANK)]
+        load_scales(x_plane, x_scales, 0)
         load_scales(w_plane0, w_scales, 0)
         x_codes.extend(load_fp4("x_codes1", x_words, 1, 2, 0, M))
         w_codes[0].extend(load_fp4("w_codes01", w_words, 1, 2, 0, BANK))
@@ -90,10 +91,11 @@ def tile_fp4_base_lowrank_fix_s4_kernel(
         b_codes = load_b("b_codes0", 0, 2 * BANK)
         load_scales(b_plane, b_scales, 0)
         bias_head = load_spread("bias_head", bias, 0, 2 * BANK)
-        load_scales(w_plane_rest, w_scales, 2 * BANK)
+        load_scales(w_plane2, w_scales, 2 * BANK)
         w_codes.append(load_fp4("w_codes2", w_words, 0, PASSES, 2 * BANK, BANK))
         b_codes.extend(load_b("b_codes2", 2 * BANK, 2 * BANK))
         bias_rest = load_spread("bias_rest", bias, 2 * BANK, N - 2 * BANK)
+        load_scales(w_plane_rest, w_scales, 3 * BANK)
         w_codes.append(load_fp4("w_codes3", w_words, 0, PASSES, 3 * BANK, BANK))
         w_codes.append(load_fp4("w_codes4", w_words, 0, PASSES, 4 * BANK, BANK))
         b_codes.extend(load_b("b_codes4", 4 * BANK, 2 * BANK))
@@ -104,7 +106,9 @@ def tile_fp4_base_lowrank_fix_s4_kernel(
                 return w_plane0[:, g, :]
             if n == 1:
                 return w_plane1[:, g, :]
-            return w_plane_rest[:, g, (n - 2) * BANK : (n - 1) * BANK]
+            if n == 2:
+                return w_plane2[:, g, :]
+            return w_plane_rest[:, g, (n - 3) * BANK : (n - 2) * BANK]
 
         def bias_cols(n):
             if n < 2:
@@ -123,6 +127,18 @@ def tile_fp4_base_lowrank_fix_s4_kernel(
                 rhs_scale=w_scale(n, g)[:, c0:c1],
                 start=(g == 0),
                 stop=False,
+            )
+
+        warm = bank(7)
+        for i in range(3):
+            nc.tensor.matmul_mx(
+                out=warm[:],
+                lhsT=x_codes[0][:, 0 : 2 * P].bitcast(FP4X4),
+                lhsT_scale=x_plane[:, 0, 0:P],
+                rhs=x_codes[0].bitcast(FP4X4),
+                rhs_scale=x_plane[:, 0, :],
+                start=(i == 0),
+                stop=(i == 2),
             )
 
         accs = {}

@@ -16,11 +16,19 @@ ALU = mybir.AluOpType
 
 P = 128
 PACK = 4
+FP4_BYTES = 2
+FP8_BYTES = 4
+QUADRANT = 32
+SCALE_ROWS = 4
 PASSES = K // (P * PACK)
 TOKEN_TILES = M // P
 BANK = 512
+BANKS = 8
 CHUNKS = N // BANK
 HALF = M // 2
+RESULT_BUFS = 16
+WARM_PASSES = 3
+LAST_TILE_CUTS = (0, 256, 384, 512)
 
 
 def tile_fp4_base_lowrank_fix_s4_kernel(
@@ -30,7 +38,7 @@ def tile_fp4_base_lowrank_fix_s4_kernel(
 
     with ExitStack() as ctx:
         keep = ctx.enter_context(tc.tile_pool(name="keep", bufs=1))
-        stage = ctx.enter_context(tc.tile_pool(name="stage", bufs=16))
+        stage = ctx.enter_context(tc.tile_pool(name="stage", bufs=RESULT_BUFS))
         psum = ctx.enter_context(tc.psum_pool(name="psum", bufs=1))
         ctx.enter_context(tc.manual_schedule())
 
@@ -41,26 +49,52 @@ def tile_fp4_base_lowrank_fix_s4_kernel(
 
         def load_scales(plane, scales, col0):
             width = plane.shape[2]
-            rows = scales[:, :, col0 : col0 + width].bitcast(I32).rearrange("g (q r) n -> r q g n", r=4)
-            for r in range(4):
-                nc.sync.dma_start(out=plane[r:P:32, :, :].bitcast(I32), in_=rows[r])
+            rows = scales[:, :, col0 : col0 + width].bitcast(I32).rearrange("g (q r) n -> r q g n", r=SCALE_ROWS)
+            for r in range(SCALE_ROWS):
+                nc.sync.dma_start(out=plane[r:P:QUADRANT, :, :].bitcast(I32), in_=rows[r])
 
         def load_fp4(name, words, g0, g1, col0, width):
-            codes = keep.tile([P, g1 - g0, 2 * width], U8, name=name, align_bytes=256)
-            src = words[g0:g1, :, 2 * col0 : 2 * (col0 + width)].bitcast(I32).rearrange("g p n -> p g n")
-            nc.sync.dma_start(out=codes[:].bitcast(I32), in_=src)
+            codes = keep.tile([P, g1 - g0, FP4_BYTES * width], U8, name=name, align_bytes=256)
+            src = words[g0:g1, :, FP4_BYTES * col0 : FP4_BYTES * (col0 + width)]
+            nc.sync.dma_start(out=codes[:].bitcast(I32), in_=src.bitcast(I32).rearrange("g p n -> p g n"))
             return [codes[:, g, :] for g in range(g1 - g0)]
 
-        def load_b(name, col0, width):
-            codes = keep.tile([P, width], U32, name=name, align_bytes=256)
-            src = b_words[0].rearrange("p n t -> p (n t)")[:, 4 * col0 : 4 * (col0 + width)].bitcast(I32)
-            nc.sync.dma_start(out=codes[:].bitcast(I32), in_=src)
-            return [codes[:, c : c + BANK] for c in range(0, width, BANK)]
+        def load_w_chunk(n):
+            return load_fp4("w_codes%d" % n, w_words, 0, PASSES, n * BANK, BANK)
 
-        def load_spread(name, vector, col0, width):
-            spread = keep.tile([P, width], BF16, name=name, align_bytes=256)
-            nc.sync.dma_start(out=spread[:], in_=vector[col0 : col0 + width].partition_broadcast(P))
-            return spread
+        def load_b_chunks(n):
+            codes = keep.tile([P, 2 * BANK], U32, name="b_codes%d" % n, align_bytes=256)
+            src = b_words[0].rearrange("p n t -> p (n t)")[:, FP8_BYTES * n * BANK : FP8_BYTES * (n + 2) * BANK]
+            nc.sync.dma_start(out=codes[:].bitcast(I32), in_=src.bitcast(I32))
+            return [codes[:, 0:BANK], codes[:, BANK : 2 * BANK]]
+
+        def load_quadrants(name, vector):
+            pairs = vector.bitcast(F32)
+            width = pairs.shape[0] // QUADRANT
+            rows = keep.tile([P, width], F32, name=name, align_bytes=64)
+            src = pairs.rearrange("(i c) -> i c", c=width).unsqueeze(0).to_broadcast([P // QUADRANT, QUADRANT, width])
+            nc.sync.dma_start(out=rows[:], in_=src)
+            return rows
+
+        def turn(name, rows, step):
+            width = rows.shape[1]
+            repeated = keep.tile([P, width, QUADRANT], F32, name=name + "_repeated", align_bytes=64)
+            turned = keep.tile([P, width, QUADRANT], F32, name=name + "_turned", align_bytes=64)
+            for c in range(0, width, step):
+                nc.scalar.copy(
+                    out=repeated[:, c : c + step, :],
+                    in_=rows[:, c : c + step].unsqueeze(2).to_broadcast([P, step, QUADRANT]),
+                )
+                nc.vector.transpose(
+                    out=turned[:, c : c + step, :].rearrange("p c i -> p (c i)"),
+                    in_=repeated[:, c : c + step, :].rearrange("p c j -> p (c j)"),
+                )
+            return turned
+
+        def put_in_order(name, turned):
+            spread = keep.tile([P, QUADRANT, turned.shape[1]], F32, name=name, align_bytes=64)
+            nc.scalar.copy(out=spread[:], in_=turned[:].rearrange("p c i -> p i c"))
+            return spread[:].rearrange("p i c -> p (i c)").bitcast(BF16)
 
         x_plane = scale_plane("x_plane", PASSES, M)
         w_plane0 = scale_plane("w_plane0", PASSES, BANK)
@@ -69,51 +103,43 @@ def tile_fp4_base_lowrank_fix_s4_kernel(
         b_plane = scale_plane("b_plane", 1, N)
         w_plane2 = scale_plane("w_plane2", PASSES, BANK)
         w_plane_rest = scale_plane("w_plane_rest", PASSES, N - 3 * BANK)
+        w_planes = [w_plane0[:], w_plane1[:], w_plane2[:]]
+        w_planes.extend(w_plane_rest[:, :, c : c + BANK] for c in range(0, N - 3 * BANK, BANK))
 
         x_codes = load_fp4("x_codes0", x_words, 0, 1, 0, M)
         w_codes = [load_fp4("w_codes00", w_words, 0, 1, 0, BANK)]
         load_scales(x_plane, x_scales, 0)
+        alpha_rows = load_quadrants("alpha_rows", alpha)
+        bias_rows = load_quadrants("bias_rows", bias)
         load_scales(w_plane0, w_scales, 0)
         x_codes.extend(load_fp4("x_codes1", x_words, 1, 2, 0, M))
         w_codes[0].extend(load_fp4("w_codes01", w_words, 1, 2, 0, BANK))
         x_codes.extend(load_fp4("x_codes2", x_words, 2, PASSES, 0, M))
         w_codes[0].extend(load_fp4("w_codes02", w_words, 2, PASSES, 0, BANK))
 
-        a_raw = keep.tile([P, PASSES, 2 * R], U8, name="a_raw", align_bytes=256)
+        a_raw = keep.tile([P, PASSES, FP4_BYTES * R], U8, name="a_raw", align_bytes=256)
         nc.sync.dma_start(out=a_raw[:].bitcast(I32), in_=a_words.bitcast(I32).rearrange("g p n -> p g n"))
         load_scales(a_plane_raw, a_scales, 0)
         sigma_bf = keep.tile([P, PACK], BF16, name="sigma_bf")
         nc.sync.dma_start(out=sigma_bf[:], in_=sigma.rearrange("(p t) -> p t", t=PACK))
-        alpha_all = load_spread("alpha_all", alpha, 0, M)
 
-        w_codes.append(load_fp4("w_codes1", w_words, 0, PASSES, BANK, BANK))
+        w_codes.append(load_w_chunk(1))
         load_scales(w_plane1, w_scales, BANK)
-        b_codes = load_b("b_codes0", 0, 2 * BANK)
+        b_codes = load_b_chunks(0)
         load_scales(b_plane, b_scales, 0)
-        bias_head = load_spread("bias_head", bias, 0, 2 * BANK)
         load_scales(w_plane2, w_scales, 2 * BANK)
-        w_codes.append(load_fp4("w_codes2", w_words, 0, PASSES, 2 * BANK, BANK))
-        b_codes.extend(load_b("b_codes2", 2 * BANK, 2 * BANK))
-        bias_rest = load_spread("bias_rest", bias, 2 * BANK, N - 2 * BANK)
+        w_codes.append(load_w_chunk(2))
+        b_codes.extend(load_b_chunks(2))
         load_scales(w_plane_rest, w_scales, 3 * BANK)
-        w_codes.append(load_fp4("w_codes3", w_words, 0, PASSES, 3 * BANK, BANK))
-        w_codes.append(load_fp4("w_codes4", w_words, 0, PASSES, 4 * BANK, BANK))
-        b_codes.extend(load_b("b_codes4", 4 * BANK, 2 * BANK))
-        w_codes.append(load_fp4("w_codes5", w_words, 0, PASSES, 5 * BANK, BANK))
+        w_codes.append(load_w_chunk(3))
+        w_codes.append(load_w_chunk(4))
+        b_codes.extend(load_b_chunks(4))
+        w_codes.append(load_w_chunk(5))
 
-        def w_scale(n, g):
-            if n == 0:
-                return w_plane0[:, g, :]
-            if n == 1:
-                return w_plane1[:, g, :]
-            if n == 2:
-                return w_plane2[:, g, :]
-            return w_plane_rest[:, g, (n - 3) * BANK : (n - 2) * BANK]
-
-        def bias_cols(n):
-            if n < 2:
-                return bias_head[:, n * BANK : (n + 1) * BANK]
-            return bias_rest[:, (n - 2) * BANK : (n - 1) * BANK]
+        alpha_turned = turn("alpha", alpha_rows, 8)
+        bias_turned = turn("bias", bias_rows, 16)
+        alpha_all = put_in_order("alpha_all", alpha_turned)
+        bias_all = put_in_order("bias_all", bias_turned)
 
         def bank(index):
             return psum.tile([P, BANK], F32, name="bank%d" % index, tag="bank%d" % index)
@@ -121,24 +147,24 @@ def tile_fp4_base_lowrank_fix_s4_kernel(
         def base_pass(acc, n, m, g, c0, c1):
             nc.tensor.matmul_mx(
                 out=acc[:, 0 : c1 - c0],
-                lhsT=x_codes[g][:, 2 * m * P : 2 * (m + 1) * P].bitcast(FP4X4),
+                lhsT=x_codes[g][:, FP4_BYTES * m * P : FP4_BYTES * (m + 1) * P].bitcast(FP4X4),
                 lhsT_scale=x_plane[:, g, m * P : (m + 1) * P],
-                rhs=w_codes[n][g][:, 2 * c0 : 2 * c1].bitcast(FP4X4),
-                rhs_scale=w_scale(n, g)[:, c0:c1],
+                rhs=w_codes[n][g][:, FP4_BYTES * c0 : FP4_BYTES * c1].bitcast(FP4X4),
+                rhs_scale=w_planes[n][:, g, c0:c1],
                 start=(g == 0),
                 stop=False,
             )
 
-        warm = bank(7)
-        for i in range(3):
+        warm = bank(BANKS - 1)
+        for i in range(WARM_PASSES):
             nc.tensor.matmul_mx(
                 out=warm[:],
-                lhsT=x_codes[0][:, 0 : 2 * P].bitcast(FP4X4),
+                lhsT=x_codes[0][:, 0 : FP4_BYTES * P].bitcast(FP4X4),
                 lhsT_scale=x_plane[:, 0, 0:P],
                 rhs=x_codes[0].bitcast(FP4X4),
                 rhs_scale=x_plane[:, 0, :],
                 start=(i == 0),
-                stop=(i == 2),
+                stop=(i == WARM_PASSES - 1),
             )
 
         accs = {}
@@ -151,16 +177,16 @@ def tile_fp4_base_lowrank_fix_s4_kernel(
         sigma_col = keep.tile([P, PACK], F32, name="sigma_col")
         a_codes, a_planes = [], []
         for t in range(PACK):
-            codes = keep.tile([P, PASSES, P, 2], U8, name="a_codes%d" % t, align_bytes=256)
-            plane = keep.tile([P, PASSES, P], U8, name="a_plane%d" % t, align_bytes=256)
+            a_words_t = keep.tile([P, PASSES, P, FP4_BYTES], U8, name="a_codes%d" % t, align_bytes=256)
+            a_plane_t = keep.tile([P, PASSES, P], U8, name="a_plane%d" % t, align_bytes=256)
             nc.vector.tensor_copy(
-                out=codes[:], in_=a_raw[:].rearrange("p g (m t b) -> p t g m b", t=PACK, b=2)[:, t]
+                out=a_words_t[:], in_=a_raw[:].rearrange("p g (j t b) -> p t g j b", t=PACK, b=FP4_BYTES)[:, t]
             )
             nc.vector.tensor_copy(
-                out=plane[:], in_=a_plane_raw[:].rearrange("p g (m t) -> p t g m", t=PACK)[:, t]
+                out=a_plane_t[:], in_=a_plane_raw[:].rearrange("p g (j t) -> p t g j", t=PACK)[:, t]
             )
-            a_codes.append(codes)
-            a_planes.append(plane)
+            a_codes.append(a_words_t)
+            a_planes.append(a_plane_t)
         nc.vector.tensor_copy(out=sigma_col[:], in_=sigma_bf[:])
 
         z_rows = keep.tile([P, PACK, M], BF16, name="z_rows", align_bytes=256)
@@ -169,7 +195,7 @@ def tile_fp4_base_lowrank_fix_s4_kernel(
             for g in range(PASSES):
                 nc.tensor.matmul_mx(
                     out=low[:],
-                    lhsT=a_codes[t][:, g].rearrange("p m b -> p (m b)").bitcast(FP4X4),
+                    lhsT=a_codes[t][:, g].rearrange("p j b -> p (j b)").bitcast(FP4X4),
                     lhsT_scale=a_planes[t][:, g, :],
                     rhs=x_codes[g].bitcast(FP4X4),
                     rhs_scale=x_plane[:, g, :],
@@ -180,48 +206,47 @@ def tile_fp4_base_lowrank_fix_s4_kernel(
                 out=z_rows[:, t, :],
                 in0=low[:],
                 scalar=sigma_col[:, t : t + 1],
-                in1=alpha_all[:],
+                in1=alpha_all,
                 op0=ALU.mult,
                 op1=ALU.mult,
             )
 
         z_grouped, z_codes, z_planes = [], [], []
-        for h in range(2):
+        for h in range(M // HALF):
             grouped = keep.tile([P, HALF, PACK], BF16, name="z_grouped%d" % h, align_bytes=256)
             nc.vector.tensor_copy(
                 out=grouped[:].rearrange("p (c i) t -> p c t i", i=4),
                 in_=z_rows[:, :, h * HALF : (h + 1) * HALF].rearrange("p t (c i) -> p c t i", i=4),
             )
             z_grouped.append(grouped)
-        for h in range(2):
-            codes = keep.tile([P, HALF], U32, name="z_codes%d" % h, align_bytes=256)
-            plane = keep.tile([P, HALF], U8, name="z_plane%d" % h, align_bytes=256)
+        for h in range(M // HALF):
+            z_words_h = keep.tile([P, HALF], U32, name="z_codes%d" % h, align_bytes=256)
+            z_plane_h = keep.tile([P, HALF], U8, name="z_plane%d" % h, align_bytes=256)
             nc.vector.quantize_mx(
-                out=codes[:].bitcast(FP8X4),
-                scales=plane[:],
-                in_=z_grouped[h][:].rearrange("p c t -> p (c t)"),
+                out=z_words_h[:].bitcast(FP8X4),
+                scales=z_plane_h[:],
+                in_=z_grouped[h][:].rearrange("p i t -> p (i t)"),
             )
-            z_codes.append(codes)
-            z_planes.append(plane)
+            z_codes.append(z_words_h)
+            z_planes.append(z_plane_h)
 
         def finish(acc, n, m, c0, c1):
             h, col = divmod(m * P, HALF)
+            out_cols = slice(n * BANK + c0, n * BANK + c1)
             nc.tensor.matmul_mx(
                 out=acc[:, 0 : c1 - c0],
                 lhsT=z_codes[h][:, col : col + P].bitcast(FP8X4),
                 lhsT_scale=z_planes[h][:, col : col + P],
                 rhs=b_codes[n][:, c0:c1].bitcast(FP8X4),
-                rhs_scale=b_plane[:, 0, n * BANK + c0 : n * BANK + c1],
+                rhs_scale=b_plane[:, 0, out_cols],
                 start=False,
                 stop=True,
             )
             result = stage.tile([P, BANK], F32, name="result", tag="result")
             nc.vector.tensor_tensor(
-                out=result[:, 0 : c1 - c0], in0=acc[:, 0 : c1 - c0], in1=bias_cols(n)[:, c0:c1], op=ALU.add
+                out=result[:, 0 : c1 - c0], in0=acc[:, 0 : c1 - c0], in1=bias_all[:, out_cols], op=ALU.add
             )
-            nc.sync.dma_start(
-                out=out[m * P : (m + 1) * P, n * BANK + c0 : n * BANK + c1], in_=result[:, 0 : c1 - c0]
-            )
+            nc.sync.dma_start(out=out[m * P : (m + 1) * P, out_cols], in_=result[:, 0 : c1 - c0])
 
         for m in range(TOKEN_TILES):
             accs[1, m] = bank(TOKEN_TILES + m)
@@ -231,11 +256,12 @@ def tile_fp4_base_lowrank_fix_s4_kernel(
             for m in range(TOKEN_TILES):
                 finish(accs[n, m], n, m, 0, BANK)
 
-        pieces = [(n, m, 0, BANK) for n in range(2, CHUNKS) for m in range(TOKEN_TILES)]
-        n, m = pieces[-1][0], pieces[-1][1]
-        pieces = pieces[:-1] + [(n, m, 0, 256), (n, m, 256, 384), (n, m, 384, 512)]
+        pieces = [(n, m, 0, BANK) for n in range(2, CHUNKS) for m in range(TOKEN_TILES)][:-1]
+        pieces.extend(
+            (CHUNKS - 1, TOKEN_TILES - 1, c0, c1) for c0, c1 in zip(LAST_TILE_CUTS[:-1], LAST_TILE_CUTS[1:])
+        )
         for index, (n, m, c0, c1) in enumerate(pieces):
-            acc = bank(index % 8)
+            acc = bank(index % BANKS)
             for g in range(PASSES):
                 base_pass(acc, n, m, g, c0, c1)
             finish(acc, n, m, c0, c1)

from contextlib import ExitStack

import concourse.mybir as mybir

M, K, N, R = 512, 2048, 3072, 512
FLOPS = 2 * M * K * N + 2 * M * K * R + 2 * M * R * N

F32 = mybir.dt.float32
BF16 = mybir.dt.bfloat16
I32 = mybir.dt.int32
U32 = mybir.dt.uint32
U8 = mybir.dt.uint8
FP4X4 = mybir.dt.float4_e2m1fn_x4
FP8X4 = mybir.dt.float8_e4m3fn_x4
ALU = mybir.AluOpType

P = 128
PACK = 4
FP4_BYTES = 2
FP8_BYTES = 4
QUADRANT = 32
SCALE_ROWS = 4
PASSES = K // (P * PACK)
TOKEN_TILES = M // P
BANK = 512
BANKS = 8
CHUNKS = N // BANK
HALF = M // 2
RESULT_BUFS = 16
WARM_PASSES = 3
LAST_TILE_CUTS = (0, 256, 384, 512)


def tile_fp4_base_lowrank_fix_s4_kernel(
    tc, x_words, x_scales, w_words, w_scales, a_words, a_scales, b_words, b_scales, sigma, alpha, bias, out
):
    nc = tc.nc

    with ExitStack() as ctx:
        keep = ctx.enter_context(tc.tile_pool(name="keep", bufs=1))
        stage = ctx.enter_context(tc.tile_pool(name="stage", bufs=RESULT_BUFS))
        psum = ctx.enter_context(tc.psum_pool(name="psum", bufs=1))
        ctx.enter_context(tc.manual_schedule())

        def scale_plane(name, passes, width):
            plane = keep.tile([P, passes, width], U8, name=name, align_bytes=256)
            nc.vector.memset(plane[:].bitcast(I32), 0)
            return plane

        def load_scales(plane, scales, col0):
            width = plane.shape[2]
            rows = scales[:, :, col0 : col0 + width].bitcast(I32).rearrange("g (q r) n -> r q g n", r=SCALE_ROWS)
            for r in range(SCALE_ROWS):
                nc.sync.dma_start(out=plane[r:P:QUADRANT, :, :].bitcast(I32), in_=rows[r])

        def load_fp4(name, words, g0, g1, col0, width):
            codes = keep.tile([P, g1 - g0, FP4_BYTES * width], U8, name=name, align_bytes=256)
            src = words[g0:g1, :, FP4_BYTES * col0 : FP4_BYTES * (col0 + width)]
            nc.sync.dma_start(out=codes[:].bitcast(I32), in_=src.bitcast(I32).rearrange("g p n -> p g n"))
            return [codes[:, g, :] for g in range(g1 - g0)]

        def load_w_chunk(n):
            return load_fp4("w_codes%d" % n, w_words, 0, PASSES, n * BANK, BANK)

        def load_b_chunks(n):
            codes = keep.tile([P, 2 * BANK], U32, name="b_codes%d" % n, align_bytes=256)
            src = b_words[0].rearrange("p n t -> p (n t)")[:, FP8_BYTES * n * BANK : FP8_BYTES * (n + 2) * BANK]
            nc.sync.dma_start(out=codes[:].bitcast(I32), in_=src.bitcast(I32))
            return [codes[:, 0:BANK], codes[:, BANK : 2 * BANK]]

        def load_quadrants(name, vector):
            pairs = vector.bitcast(F32)
            width = pairs.shape[0] // QUADRANT
            rows = keep.tile([P, width], F32, name=name, align_bytes=64)
            src = pairs.rearrange("(i c) -> i c", c=width).unsqueeze(0).to_broadcast([P // QUADRANT, QUADRANT, width])
            nc.sync.dma_start(out=rows[:], in_=src)
            return rows

        def turn(name, rows, step):
            width = rows.shape[1]
            repeated = keep.tile([P, width, QUADRANT], F32, name=name + "_repeated", align_bytes=64)
            turned = keep.tile([P, width, QUADRANT], F32, name=name + "_turned", align_bytes=64)
            for c in range(0, width, step):
                nc.scalar.copy(
                    out=repeated[:, c : c + step, :],
                    in_=rows[:, c : c + step].unsqueeze(2).to_broadcast([P, step, QUADRANT]),
                )
                nc.vector.transpose(
                    out=turned[:, c : c + step, :].rearrange("p c i -> p (c i)"),
                    in_=repeated[:, c : c + step, :].rearrange("p c j -> p (c j)"),
                )
            return turned

        def put_in_order(name, turned):
            spread = keep.tile([P, QUADRANT, turned.shape[1]], F32, name=name, align_bytes=64)
            nc.scalar.copy(out=spread[:], in_=turned[:].rearrange("p c i -> p i c"))
            return spread[:].rearrange("p i c -> p (i c)").bitcast(BF16)

        x_plane = scale_plane("x_plane", PASSES, M)
        w_plane0 = scale_plane("w_plane0", PASSES, BANK)
        a_plane_raw = scale_plane("a_plane_raw", PASSES, R)
        w_plane1 = scale_plane("w_plane1", PASSES, BANK)
        b_plane = scale_plane("b_plane", 1, N)
        w_plane2 = scale_plane("w_plane2", PASSES, BANK)
        w_plane_rest = scale_plane("w_plane_rest", PASSES, N - 3 * BANK)
        w_planes = [w_plane0[:], w_plane1[:], w_plane2[:]]
        w_planes.extend(w_plane_rest[:, :, c : c + BANK] for c in range(0, N - 3 * BANK, BANK))

        x_codes = load_fp4("x_codes0", x_words, 0, 1, 0, M)
        w_codes = [load_fp4("w_codes00", w_words, 0, 1, 0, BANK)]
        load_scales(x_plane, x_scales, 0)
        alpha_rows = load_quadrants("alpha_rows", alpha)
        bias_rows = load_quadrants("bias_rows", bias)
        load_scales(w_plane0, w_scales, 0)
        x_codes.extend(load_fp4("x_codes1", x_words, 1, 2, 0, M))
        w_codes[0].extend(load_fp4("w_codes01", w_words, 1, 2, 0, BANK))
        x_codes.extend(load_fp4("x_codes2", x_words, 2, PASSES, 0, M))
        w_codes[0].extend(load_fp4("w_codes02", w_words, 2, PASSES, 0, BANK))

        a_raw = keep.tile([P, PASSES, FP4_BYTES * R], U8, name="a_raw", align_bytes=256)
        nc.sync.dma_start(out=a_raw[:].bitcast(I32), in_=a_words.bitcast(I32).rearrange("g p n -> p g n"))
        load_scales(a_plane_raw, a_scales, 0)
        sigma_bf = keep.tile([P, PACK], BF16, name="sigma_bf")
        nc.sync.dma_start(out=sigma_bf[:], in_=sigma.rearrange("(p t) -> p t", t=PACK))

        w_codes.append(load_w_chunk(1))
        load_scales(w_plane1, w_scales, BANK)
        b_codes = load_b_chunks(0)
        load_scales(b_plane, b_scales, 0)
        load_scales(w_plane2, w_scales, 2 * BANK)
        w_codes.append(load_w_chunk(2))
        b_codes.extend(load_b_chunks(2))
        load_scales(w_plane_rest, w_scales, 3 * BANK)
        w_codes.append(load_w_chunk(3))
        w_codes.append(load_w_chunk(4))
        b_codes.extend(load_b_chunks(4))
        w_codes.append(load_w_chunk(5))

        alpha_turned = turn("alpha", alpha_rows, 8)
        bias_turned = turn("bias", bias_rows, 16)
        alpha_all = put_in_order("alpha_all", alpha_turned)
        bias_all = put_in_order("bias_all", bias_turned)

        def bank(index):
            return psum.tile([P, BANK], F32, name="bank%d" % index, tag="bank%d" % index)

        def base_pass(acc, n, m, g, c0, c1):
            nc.tensor.matmul_mx(
                out=acc[:, 0 : c1 - c0],
                lhsT=x_codes[g][:, FP4_BYTES * m * P : FP4_BYTES * (m + 1) * P].bitcast(FP4X4),
                lhsT_scale=x_plane[:, g, m * P : (m + 1) * P],
                rhs=w_codes[n][g][:, FP4_BYTES * c0 : FP4_BYTES * c1].bitcast(FP4X4),
                rhs_scale=w_planes[n][:, g, c0:c1],
                start=(g == 0),
                stop=False,
            )

        warm = bank(BANKS - 1)
        for i in range(WARM_PASSES):
            nc.tensor.matmul_mx(
                out=warm[:],
                lhsT=x_codes[0][:, 0 : FP4_BYTES * P].bitcast(FP4X4),
                lhsT_scale=x_plane[:, 0, 0:P],
                rhs=x_codes[0].bitcast(FP4X4),
                rhs_scale=x_plane[:, 0, :],
                start=(i == 0),
                stop=(i == WARM_PASSES - 1),
            )

        accs = {}
        for m in range(TOKEN_TILES):
            accs[0, m] = bank(m)
        for g in range(PASSES):
            for m in range(TOKEN_TILES):
                base_pass(accs[0, m], 0, m, g, 0, BANK)

        sigma_col = keep.tile([P, PACK], F32, name="sigma_col")
        a_codes, a_planes = [], []
        for t in range(PACK):
            a_words_t = keep.tile([P, PASSES, P, FP4_BYTES], U8, name="a_codes%d" % t, align_bytes=256)
            a_plane_t = keep.tile([P, PASSES, P], U8, name="a_plane%d" % t, align_bytes=256)
            nc.vector.tensor_copy(
                out=a_words_t[:], in_=a_raw[:].rearrange("p g (j t b) -> p t g j b", t=PACK, b=FP4_BYTES)[:, t]
            )
            nc.vector.tensor_copy(
                out=a_plane_t[:], in_=a_plane_raw[:].rearrange("p g (j t) -> p t g j", t=PACK)[:, t]
            )
            a_codes.append(a_words_t)
            a_planes.append(a_plane_t)
        nc.vector.tensor_copy(out=sigma_col[:], in_=sigma_bf[:])

        z_rows = keep.tile([P, PACK, M], BF16, name="z_rows", align_bytes=256)
        for t in range(PACK):
            low = bank(TOKEN_TILES + t)
            for g in range(PASSES):
                nc.tensor.matmul_mx(
                    out=low[:],
                    lhsT=a_codes[t][:, g].rearrange("p j b -> p (j b)").bitcast(FP4X4),
                    lhsT_scale=a_planes[t][:, g, :],
                    rhs=x_codes[g].bitcast(FP4X4),
                    rhs_scale=x_plane[:, g, :],
                    start=(g == 0),
                    stop=(g == PASSES - 1),
                )
            nc.vector.scalar_tensor_tensor(
                out=z_rows[:, t, :],
                in0=low[:],
                scalar=sigma_col[:, t : t + 1],
                in1=alpha_all,
                op0=ALU.mult,
                op1=ALU.mult,
            )

        z_grouped, z_codes, z_planes = [], [], []
        for h in range(M // HALF):
            grouped = keep.tile([P, HALF, PACK], BF16, name="z_grouped%d" % h, align_bytes=256)
            nc.vector.tensor_copy(
                out=grouped[:].rearrange("p (c i) t -> p c t i", i=4),
                in_=z_rows[:, :, h * HALF : (h + 1) * HALF].rearrange("p t (c i) -> p c t i", i=4),
            )
            z_grouped.append(grouped)
        for h in range(M // HALF):
            z_words_h = keep.tile([P, HALF], U32, name="z_codes%d" % h, align_bytes=256)
            z_plane_h = keep.tile([P, HALF], U8, name="z_plane%d" % h, align_bytes=256)
            nc.vector.quantize_mx(
                out=z_words_h[:].bitcast(FP8X4),
                scales=z_plane_h[:],
                in_=z_grouped[h][:].rearrange("p i t -> p (i t)"),
            )
            z_codes.append(z_words_h)
            z_planes.append(z_plane_h)

        def finish(acc, n, m, c0, c1):
            h, col = divmod(m * P, HALF)
            out_cols = slice(n * BANK + c0, n * BANK + c1)
            nc.tensor.matmul_mx(
                out=acc[:, 0 : c1 - c0],
                lhsT=z_codes[h][:, col : col + P].bitcast(FP8X4),
                lhsT_scale=z_planes[h][:, col : col + P],
                rhs=b_codes[n][:, c0:c1].bitcast(FP8X4),
                rhs_scale=b_plane[:, 0, out_cols],
                start=False,
                stop=True,
            )
            result = stage.tile([P, BANK], F32, name="result", tag="result")
            nc.vector.tensor_tensor(
                out=result[:, 0 : c1 - c0], in0=acc[:, 0 : c1 - c0], in1=bias_all[:, out_cols], op=ALU.add
            )
            nc.sync.dma_start(out=out[m * P : (m + 1) * P, out_cols], in_=result[:, 0 : c1 - c0])

        for m in range(TOKEN_TILES):
            accs[1, m] = bank(TOKEN_TILES + m)
            for g in range(PASSES):
                base_pass(accs[1, m], 1, m, g, 0, BANK)
        for n in range(2):
            for m in range(TOKEN_TILES):
                finish(accs[n, m], n, m, 0, BANK)

        pieces = [(n, m, 0, BANK) for n in range(2, CHUNKS) for m in range(TOKEN_TILES)][:-1]
        pieces.extend(
            (CHUNKS - 1, TOKEN_TILES - 1, c0, c1) for c0, c1 in zip(LAST_TILE_CUTS[:-1], LAST_TILE_CUTS[1:])
        )
        for index, (n, m, c0, c1) in enumerate(pieces):
            acc = bank(index % BANKS)
            for g in range(PASSES):
                base_pass(acc, n, m, g, c0, c1)
            finish(acc, n, m, c0, c1)
